import numpy as np
import ml_dtypes


def mxq(x, axis, fmt="e4m3"):
    dtype, down = {"e4m3": (ml_dtypes.float8_e4m3fn, 7), "e5m2": (ml_dtypes.float8_e5m2, 14)}[fmt]
    v = np.moveaxis(np.asarray(x, np.float32).astype(ml_dtypes.bfloat16).astype(np.float64), axis, -1)
    blocks = v.reshape(v.shape[:-1] + (-1, 32))
    amax = np.abs(blocks).max(-1, keepdims=True)
    byte = np.maximum(np.where(amax > 0, np.frexp(amax)[1] - 1 + 127, 0) - down, 1)
    scale = np.exp2(byte - 127.0)
    codes = (blocks / scale).astype(np.float32).astype(dtype).astype(np.float64)
    return np.moveaxis((codes * scale).reshape(v.shape), -1, axis)


WIDE = False


def mx_kscale(k):
    if not WIDE:
        return np.ones(k)
    levels = np.array([10, -10, 5, -5, 0])
    if k % 512:
        return np.exp2(np.random.permutation(np.resize(levels, k // 32))).repeat(32)
    a = np.empty((k // 512, 16))
    for p in range(k // 512):
        a[p, :8] = np.random.permutation(np.resize(levels, 8))
        for g in range(8):
            far = levels[np.abs(levels - a[p, g]) >= 10]
            a[p, g + 8] = far[np.random.randint(len(far))]
    return np.exp2(a.ravel()).repeat(32)


def f64(x):
    return np.asarray(x).astype(np.float64)


def striped(idx):
    return np.tile(idx.reshape(-1, 16).T, (8, 1)).astype(np.uint16)


def unstriped(offs):
    return offs[:16].T.reshape(-1).astype(np.int64)


def relu(v):
    return np.maximum(v, 0.0)


K, T, D, S, V, N = 1024, 1024, 3, 1536, 512, 128
P = 2 ** 7


def setup_inputs():
    n = np.random.standard_normal
    s = mx_kscale(K)[:, None]
    return {
        "xT": (n((K, T)) * s / np.sqrt(D)).astype(ml_dtypes.bfloat16).astype(np.float32),
        "w": (n((K, N)) / np.sqrt(K) / s).astype(np.float32),
        "b": (0.3 * n((N, 1))).astype(np.float32),
        "gate": np.tile(np.random.uniform(0.5, 1.5, (D, 1, V)), (1, P, 1)).astype(ml_dtypes.bfloat16).astype(np.float32),
        "offs": striped(np.concatenate([np.random.permutation(T)[:V] for _ in range(D)])),
    }


def reference(xT, w, b, gate, offs):
    idx = unstriped(offs)
    x = sum(f64(gate)[d, :1] * f64(xT)[:, idx[d * V:(d + 1) * V]] for d in range(D))
    return relu((mxq(f64(w), 0, "e4m3").T @ mxq(x, 0, "e4m3")) + f64(b))

from contextlib import ExitStack

import concourse.mybir as mybir
from concourse.masks import make_identity

K, T, D, V, N = 1024, 1024, 3, 512, 128
P = 128
FLOPS = 2 * K * V * N

F32 = mybir.dt.float32
BF16 = mybir.dt.bfloat16
U32 = mybir.dt.uint32
U16 = mybir.dt.uint16
U8 = mybir.dt.uint8
FP8X4 = mybir.dt.float8_e4m3fn_x4
MULT = mybir.AluOpType.mult
ADD = mybir.AluOpType.add
MAX = mybir.AluOpType.max
COPY = mybir.ActivationFunctionType.Copy
RELU = mybir.ActivationFunctionType.Relu


def tile_picked_bag_lin_relu_sub_l_kernel(tc, xT, w, b, gate, offs, out):
    nc = tc.nc
    with ExitStack() as ctx:
        keep = ctx.enter_context(tc.tile_pool(name="keep", bufs=1))
        fwd_pool = ctx.enter_context(tc.psum_pool(name="fwd", bufs=3))
        back_pool = ctx.enter_context(tc.psum_pool(name="back", bufs=3))
        acc_pool = ctx.enter_context(tc.psum_pool(name="acc", bufs=2))

        offsets = keep.tile([P, D * V // 16], U16, name="offsets")
        raw = [keep.tile([P, 2, T], F32, name=f"raw{q}") for q in range(4)]
        pairs = [keep.tile([P, 2 * T], BF16, name=f"pairs{q}") for q in range(4)]
        picked = [[keep.tile([P, 2 * V], BF16, name=f"picked{q}_{d}") for d in range(D)] for q in range(4)]
        prod = [[[keep.tile([P, 4 * P], F32, name=f"prod{c}_{d}_{j}") for j in range(4)] for d in range(D)] for c in range(2)]
        sums = [keep.tile([P, 4 * P], BF16, name=f"sums{j}") for j in range(4)]
        xb = [keep.tile([P, 4 * V], BF16, name=f"xb{c}", align_bytes=64) for c in range(2)]
        x_codes = [keep.tile([P, V], U32, name=f"x_codes{c}", align_bytes=64) for c in range(2)]
        x_scales = [keep.tile([P, V], U8, name=f"x_scales{c}", align_bytes=64) for c in range(2)]
        w_raw = keep.tile([P, 2, 4, N], F32, name="w_raw")
        wb = keep.tile([P, 2 * 4 * N], BF16, name="wb", align_bytes=64)
        w_codes = keep.tile([P, 2 * N], U32, name="w_codes", align_bytes=64)
        w_scales = keep.tile([P, 2 * N], U8, name="w_scales", align_bytes=64)
        bias = keep.tile([P, 1], F32, name="bias")
        ident = keep.tile([P, P], F32, name="ident")
        gate_rows = keep.tile([P, D, P], F32, name="gate_rows")
        gate_cols = keep.tile([P, D, 4], F32, name="gate_cols")
        warm = keep.tile([P, 2], F32, name="warm")
        result = keep.tile([P, V], F32, name="result")

        def load_x(q, t0, t1):
            c, u = divmod(q, 2)
            rows = xT[512 * c : 512 * (c + 1), :].rearrange("(p j) t -> p j t", j=4)
            nc.sync.dma_start(out=raw[q][:, :, t0:t1], in_=rows[:, 2 * u : 2 * u + 2, t0:t1])

        def cast(eng, q, t0, t1):
            dst = pairs[q][:, 2 * t0 : 2 * t1].rearrange("p (t e) -> p t e", e=2)
            src = raw[q][:, :, t0:t1].rearrange("p e t -> p t e")
            move(eng, dst, src)

        def move(eng, dst, src):
            if eng == "v":
                nc.vector.tensor_copy(out=dst, in_=src)
            elif eng == "s":
                nc.scalar.copy(out=dst, in_=src)
            else:
                nc.gpsimd.tensor_scalar(out=dst, in0=src, scalar1=1.0, scalar2=0.0, op0=MULT, op1=ADD)

        def gather(q, d, v0, v1):
            lst = offsets[:, (d * V + v0) // 16 : (d * V + v1) // 16]
            nc.vector.tensor_copy(picked[q][d][:, 2 * v0 : 2 * v1].bitcast(U32), pairs[q][:].bitcast(U32).indirect(lst))

        def turn(items):
            bank = fwd_pool.tile([P, 4 * P], F32, name="fwd_bank")
            for i, (q, d, j) in enumerate(items):
                words = picked[q][d][:, 2 * P * j : 2 * P * (j + 1)].bitcast(F32)
                nc.tensor.transpose(bank[:, i * P : (i + 1) * P], words, ident[:])
            return bank

        def weigh(bank, i, n, c, d, j, u0):
            src = bank[:, i * P : (i + n) * P].bitcast(BF16).rearrange("v (u p e) -> v u e p", u=n, e=2)
            dst = prod[c][d][j][:, 2 * P * u0 : 2 * P * (u0 + n)].rearrange("v (u e p) -> v u e p", u=n, e=2)
            nc.scalar.activation(dst, src, COPY, scale=gate_cols[:, d, j : j + 1])

        def weigh_flat(bank, i, c, d, j):
            src = bank[:, i * P : (i + 2) * P].bitcast(BF16)
            nc.scalar.activation(prod[c][d][j][:], src, COPY, scale=gate_cols[:, d, j : j + 1])

        def weigh_add(bank, i, c, d, j):
            src = bank[:, i * P : (i + 2) * P].bitcast(BF16)
            dst = sums[j] if d == D - 1 else prod[c][d][j]
            nc.vector.scalar_tensor_tensor(dst[:], src, gate_cols[:, d, j : j + 1], prod[c][d - 1][j][:], MULT, ADD)

        def back_sum(c, j):
            bank = back_pool.tile([P, 4 * P], F32, name="back_bank")
            for t in range(4):
                for d in range(D):
                    nc.tensor.matmul(bank[:, t * P : (t + 1) * P], prod[c][d][j][:, t * P : (t + 1) * P], ident[:],
                                     start=(d == 0), stop=(d == D - 1), is_transpose=True)
            return bank

        def round_out(eng, bank, c, j):
            dst = xb[c][:, 4 * P * j : 4 * P * (j + 1)].rearrange("p (v t) -> p v t", t=4)
            move(eng, dst, bank[:].rearrange("p (t v) -> p v t", t=4))

        def back_words(eng, c, j):
            bank = back_pool.tile([P, 4 * P], F32, name="back_bank")
            words = sums[j][:].bitcast(F32)
            for u in range(2):
                nc.tensor.transpose(bank[:, u * P : (u + 1) * P], words[:, u * P : (u + 1) * P], ident[:])
            dst = xb[c][:, 4 * P * j : 4 * P * (j + 1)].bitcast(F32).rearrange("p (v u) -> p v u", u=2)
            move(eng, dst, bank[:, 0 : 2 * P].rearrange("p (u v) -> p v u", u=2))

        def quant(c, v0, v1):
            nc.vector.quantize_mx(out=x_codes[c][:, v0:v1].bitcast(FP8X4), scales=x_scales[c][:, v0:v1], in_=xb[c][:, 4 * v0 : 4 * v1])

        def finish(eng, v0, v1):
            acc = acc_pool.tile([P, V], F32, name="acc")
            for c in range(2):
                nc.tensor.matmul_mx(
                    out=acc[:, 0 : v1 - v0],
                    lhsT=w_codes[:, c * N : (c + 1) * N].bitcast(FP8X4),
                    lhsT_scale=w_scales[:, c * N : (c + 1) * N],
                    rhs=x_codes[c][:, v0:v1].bitcast(FP8X4),
                    rhs_scale=x_scales[c][:, v0:v1],
                    start=(c == 0),
                    stop=(c == 1),
                )
            if eng == "s":
                nc.scalar.activation(result[:, v0:v1], acc[:, 0 : v1 - v0], RELU, bias=bias[:])
            else:
                nc.vector.tensor_scalar(out=result[:, v0:v1], in0=acc[:, 0 : v1 - v0], scalar1=bias[:], scalar2=0.0, op0=ADD, op1=MAX)
            nc.sync.dma_start(out=out[:, v0:v1], in_=result[:, v0:v1])

        def head():
            nc.vector.memset(warm[:], 0.0)
            nc.scalar.activation(warm[:, 1:2], warm[:, 0:1], RELU)
            nc.gpsimd.memset(gate_rows[:], 0.0)
            make_identity(nc, ident[:])

        def load_small():
            nc.sync.dma_start(offsets[:], offs)
            nc.sync.dma_start(out=gate_rows[0:4, :, :], in_=gate[:, 0, :].rearrange("d (j v) -> j d v", j=4))

        def load_w():
            nc.sync.dma_start(out=w_raw[:], in_=w.rearrange("(c p j) m -> p c j m", c=2, j=4))
            nc.sync.dma_start(out=bias[:], in_=b)

        def turn_gate():
            bank = fwd_pool.tile([P, 4 * P], F32, name="fwd_bank")
            for d in range(D):
                nc.tensor.transpose(bank[:, d * P : (d + 1) * P], gate_rows[:, d, :], ident[:])
            nc.scalar.copy(out=gate_cols[:], in_=bank[:, 0 : D * P].rearrange("v (d j) -> v d j", d=D)[:, :, 0:4])

        def cast_w(eng):
            move(eng, wb[:].rearrange("p (c m j) -> p c m j", c=2, j=4), w_raw[:].rearrange("p c j m -> p c m j"))

        def quant_w():
            nc.vector.quantize_mx(out=w_codes[:].bitcast(FP8X4), scales=w_scales[:], in_=wb[:])

        head()
        load_x(0, 0, 512)
        load_x(0, 512, 1024)
        load_small()
        for q in range(1, 4):
            load_x(q, 0, 512)
            load_x(q, 512, 1024)
        load_w()
        cast("v", 0, 0, 512)
        cast("v", 0, 512, 832)
        cast("s", 0, 832, 1024)
        turn_gate()
        for q in range(1, 4):
            cast("g", q, 0, 512)
            cast("g", q, 512, 1024)
        cast_w("g")
        for q in range(2):
            for d in range(D):
                gather(q, d, 0, V)
                bank = turn([(q, d, j) for j in range(4)])
                for j in range(4):
                    weigh(bank, j, 1, 0, d, j, q)
        banks = {}
        for d in range(D):
            for u in range(2):
                gather(2 + u, d, 0, 256)
        for j in range(4):
            round_out("s", back_sum(0, j), 0, j)
        for d in range(D):
            for u in range(2):
                gather(2 + u, d, 256, 512)
        for d in range(2):
            bank = turn([(2 + u, d, j) for j in range(2) for u in range(2)])
            for j in range(2):
                weigh(bank, 2 * j, 2, 1, d, j, 0)
        bank = turn([(2 + u, 0, j) for j in range(2, 4) for u in range(2)])
        for j in range(2, 4):
            weigh_flat(bank, 2 * (j - 2), 1, 0, j)
        quant_w()
        quant(0, 0, V)
        bank = turn([(2 + u, 2, j) for j in range(2) for u in range(2)])
        for j in range(2):
            weigh(bank, 2 * j, 2, 1, 2, j, 0)
        for d in range(1, D):
            bank = turn([(2 + u, d, j) for j in range(2, 4) for u in range(2)])
            for j in range(2, 4):
                weigh_add(bank, 2 * (j - 2), 1, d, j)
        for j in range(2):
            round_out("s", back_sum(1, j), 1, j)
        back_words("v", 1, 2)
        back_words("v", 1, 3)
        quant(1, 256, 512)
        finish("v", 256, 512)
        quant(1, 0, 256)
        finish("s", 0, 256)
